import numpy as np, ml_dtypes
CORES = [66,74,82,90,194,202,210,218]
N = 8
BF = ml_dtypes.bfloat16
def gentries(a):
    return np.ascontiguousarray(a.reshape(8, 16, -1).transpose(0, 2, 1)).reshape(8, -1)
def gtable(e):
    e = np.asarray(e); return np.ascontiguousarray(e.reshape(8, -1, 16).transpose(0, 2, 1)).reshape(128, -1).astype(np.int32)
NO, D, B, K, RO, TH = 16, 4, 112, 8, 4, 9
V, NB = NO * B, NO + D
def every(z):
    return np.concatenate([z, np.stack([np.roll(z[:, :, d - 1], d, axis=0) for d in range(1, D + 1)], axis=2)], axis=2)
def parts(rng):
    a = rng.integers(0, 256, (N, 8, 15, V)); m = (rng.random((N, 8, V)) < 0.0625).astype(np.int64)
    u = np.argsort(rng.random((N, 8, NB, V)), axis=-1)[..., :16 * B].reshape(N, 8, NB, 16, B)
    e = np.argsort(rng.random((N, 8, NO, B)), axis=-1)[..., :K]
    return a, m, u, np.ascontiguousarray(e)
def firsts(e):
    z = np.zeros((N, 8, V), bool); np.put_along_axis(z, (e + B * np.arange(NO)[:, None]).reshape(N, 8, -1), True, 2)
    return z
def reach(u, e):
    z = np.zeros((N, 8, V), bool); q = np.take_along_axis(u, every(e)[:, :, :, None, :], 4)
    np.put_along_axis(z, q.reshape(N, 8, -1), True, 2)
    return z
def cover(rng):
    o = np.argsort(rng.random((N, V)), axis=-1)
    return np.stack([np.roll(o, -16 * K * c, axis=1) for c in range(NB)], axis=1)
def aim(rng, e, g, o):
    ee = every(e)[:, g]; w = np.zeros((N, NB, 16, B), np.int64)
    for r in range(N):
        for c in range(NB):
            rest = np.ones(B, bool); rest[ee[r, c]] = False
            w[r, c][:, ee[r, c]] = o[r, c, :16 * K].reshape(16, K)
            w[r, c][:, rest] = rng.permutation(o[r, c, 16 * K:])[:16 * (B - K)].reshape(16, B - K)
    return w
def pack(a, m, u, e):
    rec = np.concatenate([a, m[:, :, None]], axis=2).reshape(N, 128, V).astype(np.float32).astype(BF)
    up = np.ascontiguousarray(u.transpose(0, 1, 3, 2, 4).reshape(N, 128, NB * B)).astype(np.int32)
    return {"rec": rec, "up": up, "fr": np.stack([gtable(z.reshape(8, -1)) for z in e])}
def setup_inputs(rng):
    return pack(*parts(rng))
def setup_inputs_room(rng):
    a, m, u, e = parts(rng); c = reach(u, e); z = firsts(e); can = c & ~z; pick = np.zeros((N, 8, V), bool)
    for r in range(N):
        for g in range(8):
            for b in range(NO):
                o = b * B + rng.permutation(np.flatnonzero(can[r, g, b * B:(b + 1) * B])); n = int(rng.choice(np.array([0, 1, K - 1, K, K + 1, B])))
                if r == 0 and b == 0: n = (K, K + 1, B, K - 1, 1, 0, K, K + 1)[g]
                pick[r, g, o[:n]] = True
    a = np.where(c[:, :, None], np.where(pick[:, :, None], rng.integers(150, 256, a.shape), rng.integers(0, 51, a.shape)), a)
    a = np.where(z[:, :, None], rng.integers(100, 111, a.shape), a)
    return pack(a, z.astype(np.int64), u, e)
def setup_inputs_ties(rng):
    a, m, u, e = parts(rng); z = firsts(e)
    lo = np.array([0, 254, 100, 0, 7, 127, 1, 128]).reshape(1, 8, 1, 1); step = np.array([1, 1, 1, 255, 1, 1, 2, 1]).reshape(1, 8, 1, 1)
    p = np.where(z, 0.6, 0.15 + 0.3 * rng.random((N, 8, V)))[:, :, None]
    a = lo + step * (rng.random(a.shape) < p)
    a[:, 1] = np.where((rng.random((N, V)) < 0.6)[:, None], 255, a[:, 1])
    return pack(a, m, u, e)
def setup_inputs_meet(rng):
    a, m, u, e = parts(rng)
    u[:, ::2] = u[:, ::2, :1].copy(); e[:, ::2] = e[:1, ::2, :1].copy()
    i = 1 + np.argsort(rng.random((N, 4, NO, B - 2)), axis=-1)[..., :K - 2]
    e[:, 1::2, :, 2:] = i; e[:, 1::2, :, 0] = 0; e[:, 1::2, :, 1] = B - 1
    base = np.arange(16 * B).reshape(B, 16).T; u[:, 1] = base; u[:, 1, NO:] = base + V - 16 * B
    o = np.argsort((np.arange(V) + rng.integers(0, 16, (N, 1, 1))) % 16 + rng.random((N, 1, V)), axis=-1)
    u[:, 2] = aim(rng, e, 2, np.broadcast_to(o, (N, NB, V)))[:, :1]
    u[:, 3] = aim(rng, e, 3, cover(rng)); z = firsts(e)
    a[:, 3] = np.where(z[:, 3][:, None], rng.integers(0, 51, (N, 15, V)), rng.integers(150, 256, (N, 15, V))); m[:, 3] = 0
    return pack(a, m, u, e)
def setup_inputs_dry(rng):
    a, m, u, e = parts(rng); z = firsts(e); o = rng.permutation(8)
    a[:, o[1]] = np.where(z[:, o[1]][:, None], rng.integers(100, 256, (N, 15, V)), rng.integers(0, 100, (N, 15, V)))
    for g in (o[3], o[4]):
        a[:, g] = np.where(rng.random((N, 15, V)) < 0.7, 255, rng.integers(0, 101, (N, 15, V)))
    a[:, o[3], :, ::B] = 0
    u[:, o[5]] = aim(rng, e, o[5], cover(rng))
    a[:, o[5]] = np.where(z[:, o[5]][:, None], rng.integers(0, 31, (N, 15, V)), rng.integers(80, 256, (N, 15, V)))
    a[:, o[5], :, ::B] = rng.integers(60, 101, (N, 15, NO))
    m[:, o[0]] = 1; m[:, o[2]] = rng.random((N, V)) < 0.9; m[:, o[3]] = 1; m[:, o[4]] = rng.random((N, V)) < 0.95
    m[:, o[5]] = 1; m[:, o[5], ::B] = 0
    m[(rng.integers(-2, 1) + np.arange(3)) % N] = 1
    return pack(a, m, u, e)
def setup_inputs_spread(rng):
    a, m, u, e = parts(rng); s = np.exp2(8.2 * rng.random((N, 8, 1, V)))
    a = np.minimum((s * rng.random(a.shape)).astype(np.int64), 255); m = (rng.random(m.shape) < rng.random((N, 8, 1)) * 0.5).astype(np.int64)
    return pack(a, m, u, e)
def check_inputs(d):
    bad = []
    r = d["rec"].astype(np.float32).reshape(N, 8, 16, V); a, m = r[:, :, :15], r[:, :, 15]
    if not np.all((a >= 0) & (a <= 255) & (a == np.floor(a))): bad.append("notes in rec")
    if not np.all((m == 0) | (m == 1)): bad.append("marks in rec")
    if np.min(d["up"]) < 0 or np.max(d["up"]) > V - 1: bad.append("range of up")
    u = np.sort(d["up"].reshape(N, 8, 16, NB, B).transpose(0, 1, 3, 2, 4).reshape(N, 8, NB, 16 * B), axis=-1)
    if np.any(u[..., 1:] == u[..., :-1]): bad.append("different parents in a bank of up")
    if np.min(d["fr"]) < 0 or np.max(d["fr"]) > B - 1: bad.append("range of fr")
    e = np.sort(np.stack([gentries(z) for z in d["fr"]]).reshape(N, 8, NO, K), axis=-1)
    if np.any(e[..., 1:] == e[..., :-1]): bad.append("different places in a bank of fr")
    return bad
def reference(rec, up, fr):
    s = rec.astype(np.float32).astype(np.int64).reshape(N, 8, 16, V); a = s[:, :, :15].copy(); mark = s[:, :, 15] > 0
    u = up.astype(np.int64).reshape(N, 8, 16, NB, B)
    e = np.stack([gentries(z) for z in fr]).astype(np.int64).reshape(N, 8, NO, K); live = np.ones(e.shape, bool)
    for wave in range(RO):
        node = e + B * np.arange(NO)[:, None]
        x = np.take_along_axis(a, node.reshape(N, 8, 1, NO * K), 3).reshape(N, 8, 15, NO, K)
        ee, ll, xx = every(e), every(live), every(np.moveaxis(x, 2, 3))
        new = a.copy(); hit = np.zeros((N, 8, V), bool)
        for b in range(NB):
            q = np.take_along_axis(u[:, :, :, b], ee[:, :, None, b], 3).reshape(N, 8, 1, 16 * K)
            old = np.take_along_axis(a, q, 3)
            arr = np.tile(xx[:, :, b], (1, 1, 1, 16))
            ok = (np.add.reduce((old >= arr).astype(np.int64), axis=2) >= TH) & np.tile(ll[:, :, b], (1, 1, 16))
            r, g, j = np.nonzero(ok); to = q[r, g, 0, j]
            new[r, g, :, to] = ((old + arr) >> 1)[r, g, :, j]
            hit[r, g, to] = True
        h = (hit & ~mark).reshape(N, 8, NO, B); mark = mark | hit; a = new
        e = np.argsort(~h, axis=-1, kind="stable")[..., :K]; live = np.take_along_axis(h, e, 3)
    return {"y": np.concatenate([a, mark[:, :, None].astype(np.int64)], axis=2).reshape(N, 128, V).astype(np.float32).astype(BF)}

from concourse.bass import DstId, RemoteDMATransfer
from concourse.mybir import AluOpType, ActivationFunctionType

ALU = AluOpType
ACT = ActivationFunctionType
MAGIC = 8388608.0
SCALE = 0.5 - 1.0 / 4096
WAVES = 4
CH = [(0, 2), (2, 4), (4, 6), (6, 8), (8, 12), (12, 16), (16, 20)]
GR = [[0], [1], [2, 3], [4], [5], [6]]
ORDER = ("P0 P2 P1 Q0 Q1 D0 S0 f0 f2 D1 Q2 s0 v0 S1 C0 P3 s1 K0 q3 Q5 f1 O0 S2 f3 X0 v1 D2 D3 C1 O1 v2 s2 X1 S3 s3 q4 K1 C2 O2 "
         "v3 D4 X2 s4 D5 s5 G0 S4 C3 S5 P9 C4 v4 q6 v5 O3 X3 O4 D6 X4 s6 S6 v6 C5 O5 X5")
SNAP = [("V", 0, 4), ("A", 4, 8), ("V", 8, 11), ("A", 11, 14), ("V", 14, 15), ("A", 15, 16)]
SLOT = 48

SCRATCH = {
    "UPW": ("sbuf", [128, 1920], "int32"),
    "UPG": ("sbuf", [128, 480], "int32"),
    "Bs": ("sbuf", [128, 2048], "bfloat16"),
    "F": ("sbuf", [128, 4096], "float32"),
    "Q": ("sbuf", [128, 2560], "bfloat16"),
    "SG": ("sbuf", [128, 2560], "bfloat16"),
    "VV": ("sbuf", [128, 2560], "float32"),
    "P16": ("sbuf", [128, 160], "uint16"),
    "Pf": ("sbuf", [128, 160], "float32"),
    "OFFS": ("sbuf", [128, 160], "uint16"),
    "LIST": ("sbuf", [128, 8], "uint16"),
    "LISTC": ("sbuf", [128, 8], "uint16"),
    "LISTG": ("sbuf", [128, 2], "uint16"),
    "GL": ("sbuf", [128, 16 * SLOT], "bfloat16"),
    "GN": ("sbuf", [128, 32], "bfloat16"),
    "nT": ("sbuf", [128, 128], "bfloat16"),
    "nTg": ("sbuf", [128, 128], "bfloat16"),
    "oldT": ("sbuf", [128, 128], "bfloat16"),
    "FT": ("sbuf", [128, 128], "bfloat16"),
    "OKB": ("sbuf", [128, 1024], "bfloat16"),
    "ONE": ("sbuf", [128, 128], "bfloat16"),
    "ID": ("sbuf", [128, 128], "bfloat16"),
    "IDN": ("sbuf", [128, 128], "bfloat16"),
    "DA": ("sbuf", [128, 128], "bfloat16"),
    "DB": ("sbuf", [128, 128], "bfloat16"),
    "ID2": ("sbuf", [128, 128], "float32"),
    "TRI": ("sbuf", [128, 128], "bfloat16"),
    "B1": ("sbuf", [128, 8], "bfloat16"),
    "B2": ("sbuf", [128, 8], "bfloat16"),
    "BW": ("sbuf", [128, 144], "bfloat16"),
    "SEL": ("sbuf", [128, 8], "bfloat16"),
    "EI": ("sbuf", [128, 512], "int32"),
    "EJ": ("sbuf", [128, 512], "int32"),
    "EN": ("sbuf", [128, 512], "bfloat16"),
    "EP": ("sbuf", [128, 512], "bfloat16"),
    "IP": ("sbuf", [128, 1], "int32"),
    "IT": ("sbuf", [128, 3], "int32"),
    "COL": ("sbuf", [128, 16], "float32"),
    "WV": ("sbuf", [128, 16], "float32"),
    "JB": ("sbuf", [128, 4], "float32"),
    "RW": ("sbuf", [128, 80], "bfloat16"),
    "CI": ("sbuf", [128, 18], "int32"),
    "CL": ("sbuf", [128, 10], "bfloat16"),
    "CA": ("sbuf", [128, 10], "bfloat16"),
    "CLf": ("sbuf", [128, 16], "float32"),
    "CG": ("sbuf", [128, 2], "bfloat16"),
    "FRI": ("sbuf", [128, 8], "int32"),
    "FRF": ("sbuf", [128, 8], "float32"),
    "LF": ("sbuf", [128, 16], "float32"),
}
for _w in range(WAVES):
    SCRATCH["NB%d" % _w] = ("sbuf", [128, 144], "bfloat16")
for _n in ("D0", "D1", "S0", "S1", "Y0", "Y1", "X0", "X1"):
    SCRATCH["ps" + _n] = ("psum", [128, 512], "float32")
SEMAPHORES = (["sv", "sa", "st", "sg", "lrec", "lfr", "lupg", "lsem"] + ["lup%d" % i for i in range(4)]
              + ["arr%d" % w for w in range(WAVES)] + ["out%d" % i for i in range(8)])
CSEM = {"V": "sv", "A": "sa", "T": "st", "G": "sg"}


def make_tracker(g, T):
    qs = {"V": g.vector, "A": g.scalar, "T": g.tensor, "G": g, "S": g.sync}
    known = {q: {} for q in qs}
    cnt, lw, rd, pa, seq = {}, {}, {}, {}, [0]

    def settle(q, evs):
        for ev in sorted(evs, key=lambda e: -e[4]):
            if known[q].get(ev[1], 0) >= ev[2]:
                continue
            qs[q].wait_ge(T.sem[ev[1]], ev[2])
            for s, v in ev[3].items():
                if known[q].get(s, 0) < v:
                    known[q][s] = v
            known[q][ev[1]] = ev[2]

    def op(q, call, R=(), W=(), sem=None, inc=1):
        tag = q if sem is None else "dma"
        evs = []
        for t in list(R) + list(W):
            if t[:2] == "ps":
                evs += [e for k, e in pa.get(t, {}).items() if k != tag]
        for t in R:
            if t[:2] != "ps":
                evs += lw.get(t, [])
        for t in W:
            if t[:2] != "ps":
                evs += lw.get(t, []) + list(rd.get(t, {}).values())
        settle(q, evs)
        s = CSEM[q] if sem is None else sem
        r = call(qs[q])
        for ins in (r if isinstance(r, list) else [r]):
            ins.then_inc(T.sem[s], inc)
            cnt[s] = cnt.get(s, 0) + inc
        seq[0] += 1
        ev = (tag, s, cnt[s], dict(known[q]), seq[0])
        for t in list(R) + list(W):
            if t[:2] == "ps":
                pa.setdefault(t, {})[tag] = ev
        for t in R:
            if t[:2] != "ps":
                rd.setdefault(t, {})[tag if tag != "dma" else s] = ev
        for t in W:
            if t[:2] != "ps":
                lw[t] = [ev]
                rd[t] = {}

    def arrive(t, sem, val):
        seq[0] += 1
        lw[t] = [("remote", sem, val, {}, seq[0])]

    def ready(q, toks):
        settle(q, [e for t in toks for e in lw.get(t, [])])

    def finish(extra):
        for s, v in list(cnt.items()) + extra:
            if known["G"].get(s, 0) < v:
                g.wait_ge(T.sem[s], v)
    return op, arrive, ready, finish


def rank_program(g, core, T, topo):
    rank = T.rank_of(core)
    if rank is None:
        return
    N = len(T.cores)
    op, arrive, ready, finish = make_tracker(g, T)
    BK = ["Bs%d" % b for b in range(16)]
    BS = BK + ["Bsp"]
    FF = ["Fa", "Fb"]
    last = len(CH) - 1

    def vts(out, in0, s1, s2, op0, op1, R, W):
        if op1 is None:
            op("V", lambda v: v.tensor_scalar(out, in0, s1, None, op0), R, W)
        else:
            op("V", lambda v: v.tensor_scalar(out, in0, s1, s2, op0, op1), R, W)

    def vcopy(out, in_, R, W):
        op("V", lambda v: v.tensor_copy(out, in_), R, W)

    def fill(ap, c, W):
        op("V", lambda v: v.memset(ap, c), (), W)

    def sel(out, in_, pat, cmp, base, cm, R, W):
        op("G", lambda q: q.affine_select(out, in_, pat, cmp, 0.0, base, cm), R, W)

    def iota(out, pat, base, cm, W):
        op("G", lambda q: q.iota(out, pat, base, cm), (), W)

    def iotaf(out, pat, base, cm, W):
        op("G", lambda q: q.iota(out, pat, base, cm, allow_small_or_imprecise_dtypes=True), (), W)

    def act(out, in_, R, W, scale=1.0, bias=None):
        if bias is None:
            f = ACT.Copy if isinstance(scale, float) else ACT.Identity
            op("A", lambda a: a.activation(out, in_, f, scale=scale), R, W)
        else:
            op("A", lambda a: a.activation(out, in_, ACT.Identity, bias=bias, scale=scale), R, W)

    op("S", lambda s: s.dma_start(T.FRI[:, :], T.fr[:, :]), (), ["FRI"], "lfr", 16)
    op("A", lambda s: s.dma_start(T.Bs[:, 0:1792], T.rec[:, :]), (), BK, "lrec", 16)
    for i in range(4):
        op("S", lambda s: s.dma_start(T.UPW[:, 448 * i:448 * i + 448], T.up[:, 448 * i:448 * i + 448]),
           (), ["UPW%d" % i], "lup%d" % i, 16)
    op("S", lambda s: [s.dma_start(T.UPG[:, 120 * d:120 * d + 112], T.up[:, 1792 + 112 * d:1904 + 112 * d]) for d in range(4)],
       (), ["UPG"], "lupg", 16)

    fill(T.ONE[:, :], 1.0, ["ONE"])
    iota(T.IP[:, :], [[0, 1]], 0, 1, ["IP"])
    iota(T.CI[:, 0:10], [[224, 10]], 0, 0, ["CI0"])
    iota(T.CI[:, 10:18], [[0, 4], [224, 2]], 0, 0, ["CI1"])
    iota(T.EI[:, :], [[1, 32], [0, 16]], 128, -1, ["EI"])
    sel(T.ID[:, :], T.ONE[:, :], [[-1, 128]], ALU.is_equal, 0, 1, ["ONE"], ["ID"])
    sel(T.B1[:, :], T.ONE[:, 0:8], [[-16, 8]], ALU.is_ge, 0, 1, ["ONE"], ["B1"])
    sel(T.B2[:, :], T.B1[:, :], [[16, 8]], ALU.is_ge, 14, -1, ["B1"], ["B2"])
    sel(T.SEL[:, :], T.ONE[:, 0:8], [[-16, 8]], ALU.is_equal, -15, 1, ["ONE"], ["SEL"])
    sel(T.TRI[:, :], T.ONE[:, :], [[1, 128]], ALU.is_ge, 0, -1, ["ONE"], ["TRI"])
    iotaf(T.WV[:, 0:8], [[-224, 8]], 1679, 0, ["WV0"])
    iotaf(T.WV[:, 8:16], [[-224, 8]], 1800, 0, ["WV1"])
    iotaf(T.JB[:, :], [[2, 4]], 9, 0, ["JB"])
    iota(T.UPW[:, 1792:1920], [[0, 8], [16, 16]], 1792, 1, ["UPWp"])
    for d in range(4):
        iota(T.UPG[:, 120 * d + 112:120 * d + 120], [[16, 8]], 1792, 1, ["UPGp%d" % d])
    C = lambda i: T.COL[:, i:i + 1]
    vts(T.IT[:, 1:2], T.IP[:, :], 3, 1, ALU.logical_shift_right, ALU.bitwise_and, ["IP"], ["IT1"])
    vts(T.IT[:, 0:1], T.IP[:, :], 15, None, ALU.bitwise_and, None, ["IP"], ["IT0"])
    vts(C(3), T.IT[:, 1:2], 112.0, None, ALU.mult, None, ["IT1"], ["c3"])
    vts(C(0), T.IT[:, 0:1], 14.5, None, ALU.is_lt, None, ["IT0"], ["c0"])
    vts(T.CLf[:, 0:8], T.CI[:, 0:8], C(3), None, ALU.add, None, ["CI0", "c3"], ["CLf0"])
    vts(T.CLf[:, 8:16], T.CI[:, 10:18], C(3), None, ALU.add, None, ["CI1", "c3"], ["CLf1"])
    vts(C(1), C(0), -2.0, 2.0, ALU.mult, ALU.add, ["c0"], ["c1"])
    vts(T.IT[:, 2:3], T.IP[:, :], 2, 1, ALU.logical_shift_right, ALU.bitwise_and, ["IP"], ["IT2"])
    fill(T.Bs[:, 1792:2048], 0.0, ["Bsp"])
    vcopy(T.FRF[:, :], T.FRI[:, :], ["FRI"], ["FRF"])
    op("V", lambda v: v.tensor_tensor(T.LF[:, 0:8], T.FRF[:, :], T.CLf[:, 0:8], ALU.add), ["FRF", "CLf0"], ["LF0"])
    op("V", lambda v: v.tensor_tensor(T.LF[:, 8:16], T.FRF[:, :], T.CLf[:, 8:16], ALU.add), ["FRF", "CLf1"], ["LF1"])
    vcopy(T.NB0[:, 14:16], T.FRI[:, 0:2], ["FRI"], ["NBp0"])
    vcopy(T.LIST[:, :], T.LF[:, 0:8], ["LF0"], ["LIST"])
    vcopy(T.LISTC[:, :], T.LF[:, 8:16], ["LF1"], ["LISTC"])
    vts(T.EJ[:, :], T.EI[:, :], 31, None, ALU.bitwise_and, None, ["EI"], ["EJ"])
    fill(C(8), MAGIC, ["c8"])
    fill(C(9), 0.5, ["c9"])
    fill(C(12), 1.0, ["c12"])
    fill(T.BW[:, :], 0.0, ["BW"])
    vts(T.EN[:, :], T.EJ[:, :], 0.0, -1.0, ALU.is_equal, ALU.mult, ["EJ"], ["EN"])
    act(T.IDN[:, :], T.ID[:, :], ["ID", "c0"], ["IDN"], C(0))
    act(T.ID2[:, :], T.ID[:, :], ["ID"], ["ID2"], 2.0)
    act(T.BW[:, 15:128:16], T.B2[:, :], ["B2", "BW"], ["BW"], -1.0 / 32)
    act(T.EP[:, :], T.EN[:, :], ["EN"], ["EP"], -1.0)

    def late_constants():
        vcopy(C(2), T.IT[:, 1:2], ["IT1"], ["c2"])
        vts(C(4), T.IT[:, 1:2], 120.0, None, ALU.mult, None, ["IT1"], ["c4"])
        vts(C(5), T.IT[:, 1:2], -1.0, 1.0, ALU.mult, ALU.add, ["IT1"], ["c5"])
        vts(C(7), T.IP[:, :], 120.0, None, ALU.is_equal, None, ["IP"], ["c7"])
        vts(C(10), T.IP[:, :], 120.0, None, ALU.not_equal, None, ["IP"], ["c10"])
        vcopy(C(11), T.IT[:, 2:3], ["IT2"], ["c11"])
        fill(C(13), 240.0, ["c13"])
        fill(T.CL[:, 8:10], 0.0, ["CL1"])
        fill(T.RW[:, :], 0.0, ["RW"])
        fill(T.FT[:, :], 1.0, ["FT"])
        vcopy(T.TRI[:, 120:121], T.TRI[:, 111:112], ["TRI"], ["TRI"])

    def late_scalar():
        act(T.DA[:, :], T.ID[:, :], ["ID", "c5"], ["DA"], C(5))
        act(T.DB[:, :], T.ID[:, :], ["ID", "c2"], ["DB"], C(2))
        act(T.CG[:, 0:1], C(4), ["c4"], ["CG0"])
        act(T.CG[:, 1:2], C(4), ["c4", "c13"], ["CG1"], 1.0, C(13))
        act(T.CL[:, 0:8], T.CLf[:, 0:8], ["CLf0"], ["CL0"], 2.0)
        act(T.CA[:, 0:8], T.WV[:, 8:16], ["WV1", "c11"], ["CA0"], C(11))
        act(T.CA[:, 8:9], C(11), ["c11"], ["CA1"], 120.0)
        act(T.CA[:, 9:10], C(11), ["c11"], ["CA2"], 120.0)
        act(T.RW[:, 0:80:11], T.WV[:, 0:8], ["WV0", "c7", "c12", "RW"], ["RW"], C(7), C(12))
        act(T.RW[:, 8:9], C(10), ["c10"], ["RW"])
        act(T.RW[:, 19:20], C(10), ["c10"], ["RW"])

    def marks(lo, hi):
        op("T", lambda t: [t.matmul(T.psX1[0:112, 16 * (b // 2) + b % 2:16 * (b // 2) + 16:2],
                                    T.Bs[:, 112 * b:112 * b + 112], T.SEL[:, :], True, True) for b in range(lo, hi)],
           BK[lo:hi] + ["SEL"], ["psX1"])

    def keep_marks():
        act(T.oldT[0:112, :], T.psX1[0:112, 0:128], ["psX1"], ["oldT"])

    def gather(q, i):
        a, b = CH[i]
        out, win = T.Q[:, 128 * a:128 * b], T.Bs[:, :].indirect(T.P16[:, 8 * a:8 * b])
        if q == "V":
            vcopy(out, win, BS + ["P%d" % i], ["Q%d" % i])
        else:
            act(out, win, BS + ["P%d" % i], ["Q%d" % i])

    def piece(i, kind="D"):
        bank = "ps%s%d" % (kind, i % 2)
        a, b = CH[i]
        if a < 16:
            k = a // 4 * 32
            x = 128 * (a % 4)
            return 128 * (b - a), bank, T.nT[k:k + 32, :], slice(k, k + 32), slice(x, x + 128 * (b - a)), "nT"
        return 128 * (b - a), bank, T.nTg[0:32, :], slice(0, 32), slice(0, 512), "nTg"

    def diff(i):
        n, ps, w, kr, xr, tok = piece(i)
        a = 128 * CH[i][0]
        op("T", lambda t: [t.matmul(T[ps][:, 0:n], T.IDN[:, :], T.Q[:, a:a + n], True, False),
                           t.matmul(T[ps][:, 0:n], w, T.EN[kr, xr], False, True)], ["Q%d" % i, "IDN", "EN", tok], [ps])

    def total(i):
        n, ps, w, kr, xr, tok = piece(i, "S")
        a = 128 * CH[i][0]
        op("T", lambda t: [t.matmul(T[ps][:, 0:n], T.IDN[:, :], T.Q[:, a:a + n], True, False),
                           t.matmul(T[ps][:, 0:n], w, T.EP[kr, xr], False, True)], ["Q%d" % i, "IDN", "EP", tok], [ps])

    def sign(i):
        n, ps = piece(i)[:2]
        a = 128 * CH[i][0]
        op("A", lambda s: s.activation(T.SG[:, a:a + n], T[ps][:, 0:n], ACT.Sign, bias=C(9)), [ps, "c9"], ["SG%d" % i])

    def value(i):
        n, ps = piece(i, "S")[:2]
        a = 128 * CH[i][0]
        act(T.VV[:, a:a + n], T[ps][:, 0:n], [ps, "c8"], ["VV%d" % i], SCALE, C(8))

    def cols(gi):
        return 8 * CH[GR[gi][0]][0], 8 * CH[GR[gi][-1]][1], "psY%d" % (gi % 2)

    def count(gi):
        lo, hi, ps = cols(gi)
        out = T[ps][:, 0:hi - lo]
        op("T", lambda t: [t.matmul(out, T.ID2[:, :], T.Pf[:, lo:hi], True, False)], ["ID2"] + ["Pf%d" % i for i in GR[gi]], [ps])
        op("T", lambda t: [t.matmul(out, T.BW[:, 15 - k:143 - k], T.SG[:, 16 * lo + k:16 * hi:16], False, k == 15) for k in range(16)],
           ["BW"] + ["SG%d" % i for i in GR[gi]], [ps])

    def offsets(gi):
        lo, hi, ps = cols(gi)
        vts(T.OFFS[:, lo:hi], T[ps][:, 0:hi - lo], 0.5625, None, ALU.add, None, [ps], ["OF%d" % gi])

    def scatter(gi):
        for i in GR[gi]:
            for b in range(*CH[i]):
                vts(T.F[:, :].indirect(T.OFFS[:, 8 * b:8 * b + 8]), T.VV[:, 128 * b:128 * b + 128], 1.0, -MAGIC,
                    ALU.mult, ALU.add, ["OF%d" % gi, "VV%d" % i], FF)

    def pf(i, j):
        a, b = 8 * CH[i][0], 8 * CH[j][1]
        vcopy(T.Pf[:, a:b], T.P16[:, a:b], ["P%d" % k for k in range(i, j + 1)], ["Pf%d" % k for k in range(i, j + 1)])

    def send(w):
        dst = [T.cores[(rank + d) % N] for d in range(1, 5)]
        common = [e for e in topo.engines(core, dst[0]) if all(e in topo.engines(core, c) for c in dst)]
        ne = max(x for x in (1, 2, 4, 8, 16) if x <= len(common))
        m = sum(1 << e for e in common[:ne])
        ids = []
        for c in dst:
            rid, pid = topo.addr(c, core)
            ids.append(DstId(rid=rid, pnc=pid))
        ready("G", ["NBn%d" % w, "NBp%d" % w])
        g.remote_dma_fused([RemoteDMATransfer(
            dst_ids=ids, dma_engine_mask=m, remote_sem=T.sem["arr%d" % w], srcs=[T["NB%d" % w][:, 14:48]],
            dsts=[T.GL[:, (4 * w + d) * SLOT:(4 * w + d) * SLOT + 34] for d in range(4)])], local_sem=T.sem["lsem"])
        arrive("GL%d" % w, "arr%d" % w, 4 * ne)
        return ne

    def nodes(w):
        NBt = T["NB%d" % w]
        act(NBt[:, 16:144], T.Bs[:, :].indirect(T.LIST[:, :]), BS + ["LIST", "c0", "c1"], ["NBn%d" % w], C(0), C(1))
        op("T", lambda t: [t.matmul(T.psX0[:, 0:128], NBt[:, 16:144], T.ID[:, :], True, True)], ["NBn%d" % w, "ID"], ["psX0"])
        act(T.nT[:, :], T.psX0[:, 0:128], ["psX0"], ["nT"])

    def ghosts_in(w):
        for d in range(4):
            s = (4 * w + d) * SLOT + 2 + 8 * d
            sel(T.GN[:, 8 * d:8 * d + 8], T.GL[:, s:s + 8], [[0, 8]], ALU.is_gt, 1, 0, ["GL%d" % w], ["GN%d" % d])

    def ghosts_list(w):
        def mm(t):
            r = []
            for x in range(2):
                o = T.psX1[:, x:x + 1]
                s = (4 * w + 2 * x) * SLOT + x
                r += [t.matmul(o, T.ID[:, :], T.CG[:, x:x + 1], True, False), t.matmul(o, T.DA[:, :], T.GL[:, s:s + 1], False, False),
                      t.matmul(o, T.DB[:, :], T.GL[:, s + SLOT:s + SLOT + 1], False, True)]
            return r
        op("T", mm, ["ID", "DA", "DB", "CG0", "CG1", "GL%d" % w], ["psX1"])

    def ghosts_nT():
        op("T", lambda t: [t.matmul(T.psX0[0:32, 0:128], T.GN[:, :], T.ID[:, :], True, True)],
           ["ID"] + ["GN%d" % d for d in range(4)], ["psX0"])
        act(T.nTg[0:32, :], T.psX0[0:32, 0:128], ["psX0"], ["nTg"])

    def ghosts_parents():
        vcopy(T.LISTG[:, :], T.psX1[:, 0:2], ["psX1"], ["LISTG"])
        vcopy(T.P16[:, 128:160], T.UPG[:, :].indirect(T.LISTG[:, :]), ["LISTG", "UPG"] + ["UPGp%d" % d for d in range(4)], ["P%d" % last])
        pf(last, last)

    def snap(q, lo, hi):
        out, in_ = T.Bs[:, 112 * lo:112 * hi], T.F[:, 224 * lo:224 * hi:2]
        if q == "V":
            vcopy(out, in_, FF, BK[lo:hi])
        else:
            act(out, in_, FF, BK[lo:hi])

    def frontier(w):
        op("T", lambda t: [t.matmul(T.psX0[:, 0:10], T.ID[:, :], T.CL[:, :], True, False),
                           t.matmul(T.psX0[:, 0:10], T.ID[:, :], T.CA[:, :], False, False)],
           ["ID", "CL0", "CL1", "CA0", "CA1", "CA2"], ["psX0"])
        for q, lo, hi in SNAP:
            snap(q, lo, hi)
        for q, lo, hi in SNAP:
            marks(lo, hi)
        op("V", lambda v: v.tensor_tensor(T.FT[0:112, :], T.psX1[0:112, 0:128], T.oldT[0:112, :], ALU.subtract), ["psX1", "oldT"], ["FT"])
        for ps in ("psY0", "psY1"):
            op("T", lambda t: [t.matmul(T[ps][0:121, 0:128], T.TRI[0:120, 0:121], T.FT[0:120, :], True, True)], ["TRI", "FT"], [ps])
        for j in range(4):
            vts(T.OKB[0:121, j:1024:8], T.psY0[0:121, 0:128], j + 0.5, 2.0, ALU.is_lt, ALU.mult, ["psY0"], ["OK%d" % j])
            op("A", lambda a: a.activation(T.OKB[0:121, j + 4:1024:8], T.psY1[0:121, 0:128], ACT.Sign, bias=T.JB[0:121, j:j + 1], scale=-2.0),
               ["psY1", "JB"], ["OK%d" % (j + 4)])
        keep_marks()
        op("T", lambda t: [t.matmul(T.psX0[:, 0:10], T.OKB[0:121, 128 * c:128 * c + 128], T.RW[0:121, 10 * c:10 * c + 10], False, c == 7)
                           for c in range(8)], ["RW"] + ["OK%d" % j for j in range(8)], ["psX0"])
        vts(T.LIST[:, :], T.psX0[:, 0:8], 0.5, None, ALU.mult, None, ["psX0"], ["LIST"])
        act(T["NB%d" % (w + 1)][:, 14:16], T.psX0[:, 8:10], ["psX0"], ["NBp%d" % (w + 1)], 0.5)

    def steps(text, w):
        one = {"Q": lambda n: gather("V", n), "q": lambda n: gather("A", n), "D": diff, "s": sign, "S": total, "v": value,
               "C": count, "O": offsets, "X": scatter}
        for t in text.split():
            n = int(t[1:])
            if t[0] in one:
                one[t[0]](n)
            elif t[0] == "G":
                ghosts_in(w)
                ghosts_list(w)
                ghosts_nT()
            elif t == "P9":
                ghosts_parents()
            elif t[0] in "Pf":
                ks = [k for k in range(last) if CH[k][0] // 4 == n] if w == 0 else list(range(last))
                if w and n:
                    continue
                if t[0] == "f":
                    pf(ks[0], ks[-1])
                elif w == 0:
                    vcopy(T.P16[:, 32 * n:32 * n + 32], T.UPW[:, 448 * n:448 * n + 448].indirect(T.LISTC[:, 2 * n:2 * n + 2]),
                          ["LISTC", "UPW%d" % n], ["P%d" % k for k in ks])
                else:
                    vcopy(T.P16[:, 0:128], T.UPW[:, :].indirect(T.LIST[:, :]), ["LIST", "UPWp"] + ["UPW%d" % i for i in range(4)],
                          ["P%d" % k for k in ks])
            elif w == 0 and t == "K0":
                vcopy(T.F[:, 0:896:2], T.Bs[:, 0:448], BK[0:4], ["Fa"])
                late_constants()
            elif w == 0 and t == "K1":
                marks(0, 16)
                keep_marks()
                late_scalar()

    ne = 0
    for w in range(WAVES):
        nodes(w)
        if w == 0:
            act(T.F[:, 896:3584:2], T.Bs[:, 448:1792], BK[4:16], ["Fb"])
        ne = send(w)
        steps(ORDER, w)
        if w + 1 < WAVES:
            frontier(w)
    for k, (q, lo, hi) in enumerate(SNAP):
        snap(q, lo, hi)
        op("S" if q == "V" else "A", lambda s: s.dma_start(T.y[:, 112 * lo:112 * hi], T.Bs[:, 112 * lo:112 * hi]),
           BK[lo:hi], ["y%d" % k], "out%d" % k, 16)
    finish([("lsem", ne * WAVES)] + [("arr%d" % w, 4 * ne) for w in range(WAVES)])
